import numpy as np
import ml_dtypes


def mxq(x, axis, fmt="e4m3"):
    dtype, down = {"e4m3": (ml_dtypes.float8_e4m3fn, 7), "e5m2": (ml_dtypes.float8_e5m2, 14)}[fmt]
    v = np.moveaxis(np.asarray(x, np.float32).astype(ml_dtypes.bfloat16).astype(np.float64), axis, -1)
    blocks = v.reshape(v.shape[:-1] + (-1, 32))
    amax = np.abs(blocks).max(-1, keepdims=True)
    byte = np.maximum(np.where(amax > 0, np.frexp(amax)[1] - 1 + 127, 0) - down, 1)
    scale = np.exp2(byte - 127.0)
    codes = (blocks / scale).astype(np.float32).astype(dtype).astype(np.float64)
    return np.moveaxis((codes * scale).reshape(v.shape), -1, axis)


WIDE = False


def mx_kscale(k):
    if not WIDE:
        return np.ones(k)
    levels = np.array([10, -10, 5, -5, 0])
    if k % 512:
        return np.exp2(np.random.permutation(np.resize(levels, k // 32))).repeat(32)
    a = np.empty((k // 512, 16))
    for p in range(k // 512):
        a[p, :8] = np.random.permutation(np.resize(levels, 8))
        for g in range(8):
            far = levels[np.abs(levels - a[p, g]) >= 10]
            a[p, g + 8] = far[np.random.randint(len(far))]
    return np.exp2(a.ravel()).repeat(32)


BF16 = ml_dtypes.bfloat16


def bf(x):
    return np.asarray(x, np.float32).astype(BF16)


def f64(x):
    return np.asarray(x).astype(np.float64)


E2M1 = np.array([0.0, 0.5, 1.0, 1.5, 2.0, 3.0, 4.0, 6.0, -0.0, -0.5, -1.0, -1.5, -2.0, -3.0, -4.0, -6.0])


def pack_weight(w, fmt):
    k, n = w.shape
    w = f64(bf(w)).reshape(k // 32, 32, n)
    amax = np.abs(w).max(1)
    if fmt == "e4m3":
        byte = np.frexp(amax)[1] - 1 + 127 - 7
    else:
        mant, ex = np.frexp(amax / 6.0)
        byte = np.where(mant > 0.5, ex, ex - 1) + 127
    byte = np.clip(np.where(amax > 0, byte, 1), 1, 254)
    scaled = (w * np.exp2(127.0 - byte)[:, None, :]).reshape(k, n).astype(np.float32)
    by_word = np.ascontiguousarray(scaled.reshape(k // 512, 128, 4, n).transpose(0, 1, 3, 2))
    if fmt == "e4m3":
        words = by_word.astype(ml_dtypes.float8_e4m3fn).view(np.uint8)
    else:
        c = by_word.astype(ml_dtypes.float4_e2m1fn).view(np.uint8) & 0xF
        words = c[..., 0::2] | (c[..., 1::2] << 4)
    return np.ascontiguousarray(words), np.ascontiguousarray(byte.astype(np.uint8).reshape(k // 512, 16, n))


def unpack_weight(words, scales, fmt):
    g, p, n, _ = words.shape
    if fmt == "e4m3":
        vals = np.ascontiguousarray(words).view(ml_dtypes.float8_e4m3fn).astype(np.float64)
    else:
        nib = np.empty((g, p, n, 4), np.uint8)
        nib[..., 0::2] = words & 0xF
        nib[..., 1::2] = words >> 4
        vals = E2M1[nib]
    vals = vals * np.repeat(np.exp2(scales.astype(np.float64) - 127.0), 8, axis=1)[..., None]
    return vals.transpose(0, 1, 3, 2).reshape(g * 512, n)
def pack4(w):
    words, scales = pack_weight(w, "e2m1")
    return words.reshape(words.shape[0], 128, -1), scales


def unpack4(words, scales):
    return unpack_weight(words.reshape(words.shape[0], 128, -1, 2), scales, "e2m1")


def planes(Y):
    n, m = Y.shape
    b = f64(bf(Y)).reshape(n // 32, 32, m)
    amax = np.abs(b).max(1)
    byte = np.clip(np.where(amax > 0, np.frexp(amax)[1] - 1 + 127 - 7, 1), 1, 254)
    codes = (b * np.exp2(127.0 - byte)[:, None, :]).reshape(n, m).astype(np.float32).astype(ml_dtypes.float8_e4m3fn).view(np.uint8)
    words = codes.reshape(n // 512, 128, 4, m).transpose(0, 1, 3, 2)
    return np.ascontiguousarray(words), np.ascontiguousarray(byte.astype(np.uint8).reshape(n // 512, 16, m))


H, T, D, S = 40, 32, 512, 3072

def setup_inputs():
    s = mx_kscale(D)
    q = bf(np.random.randn(H, T, D) * s)
    length = np.exp(0.3 * np.random.randn(1, S))
    keys = np.random.randn(D, S) / np.sqrt(D) * length / s[:, None]
    keys_words, keys_scales = pack4(keys)
    scale = bf(np.exp(0.3 * np.random.randn(H)))
    age = 1.0 - np.arange(S) / S
    offset = -1.0 + 0.5 * np.random.randn(H, 1) - 2.5 * np.random.rand(H, 1) * age[None, :]
    offset = bf(offset + 0.8 * np.random.randn(H, S))
    return {"q": q, "keys_words": keys_words, "keys_scales": keys_scales,
            "scale": scale, "offset": offset}

def reference(q, keys_words, keys_scales, scale, offset):
    qq = mxq(f64(q).reshape(H * T, D), 1, "e4m3")
    C = unpack4(keys_words, keys_scales)
    scores = (qq @ C).reshape(H, T, S)
    z = scores * f64(scale)[:, None, None] + f64(offset)[:, None, :]
    w = 1.0 / (1.0 + np.exp(-z))
    seen = np.arange(S)[None, :] <= S - T + np.arange(T)[:, None]
    y = np.where(seen[None, :, :], w, 0.0)
    Y = y.reshape(H * T, S).T
    words, scales = planes(Y)
    return y, words, scales

@@ -1,0 +1,283 @@
+from contextlib import ExitStack
+
+import concourse.mybir as mybir
+from concourse.masks import make_identity
+
+H, T, D, S = 40, 32, 512, 3072
+M = H * T
+FLOPS = 2 * M * D * S
+
+F32 = mybir.dt.float32
+BF16 = mybir.dt.bfloat16
+I32 = mybir.dt.int32
+U32 = mybir.dt.uint32
+U8 = mybir.dt.uint8
+FP8X4 = mybir.dt.float8_e4m3fn_x4
+FP4X4 = mybir.dt.float4_e2m1fn_x4
+ALU = mybir.AluOpType
+ACT = mybir.ActivationFunctionType
+
+P = 128
+CHUNK = 512
+N_CHUNKS = S // CHUNK
+PAIRS = 5
+STEPS = N_CHUNKS * PAIRS
+M_WIDE = 1024
+CHUNK_ORDER = [4, 5, 0, 1, 2, 3]
+STEP_PLAN = [(s // 2, s % 2) for s in range(2 * PAIRS)] + [(s % PAIRS, s // PAIRS) for s in range(2 * PAIRS, STEPS)]
+MASKED = -(2.0 ** 126)
+SCORE_LEAD = 2
+TURN_LAG = 3
+SCALAR_COPY_LAG = 4
+VECTOR_COPY_LAG = 5
+VECTOR_ROUND_LAG = 3
+QUANT_LAG = 8
+VECTOR_EVAC = range(1, 24, 4)
+VECTOR_CAST = range(STEPS - 3, STEPS)
+WINDOWS = [(6, 0, 1024), (8, 1024, 1024), (13, 2048, 1024), (18, 3072, 1024), (19, 4096, 1024),
+           (23, 5120, 1024), (24, 6144, 256), (28, 6400, 1024), (29, 7424, 256)]
+
+
+def pair_rows(rows, pair):
+    if pair < PAIRS - 1:
+        return rows[0:M_WIDE, :].rearrange("(p c) n -> p c n", c=8)[:, 2 * pair : 2 * pair + 2, :]
+    return rows[M_WIDE:M, :].rearrange("(p c) n -> p c n", c=2)
+
+
+def tile_causal_sigmoid_attention_weights_g4_kernel(
+    tc, q, keys_words, keys_scales, scale, offset, out_0, out_1, out_2
+):
+    nc = tc.nc
+    q_rows = q.rearrange("h i d -> (h i) d")
+    y_rows = out_0.rearrange("h i j -> (h i) j")
+
+    with ExitStack() as ctx:
+        keep = ctx.enter_context(tc.tile_pool(name="keep", bufs=1))
+        work = ctx.enter_context(tc.tile_pool(name="work", bufs=1))
+        psum = ctx.enter_context(tc.psum_pool(name="psum", bufs=1))
+        ctx.enter_context(tc.manual_schedule())
+
+        ident = keep.tile([P, P], F32, name="ident")
+        warm = keep.tile([P, 1], F32, name="warm")
+        warm_out = keep.tile([P, 1], F32, name="warm_out")
+        k_codes = keep.tile([P, 2 * S], U8, name="k_codes", align_bytes=64)
+        k_scales = keep.tile([P, S], U8, name="k_scales", align_bytes=64)
+        q_raw = [keep.tile([P, 2, D], BF16, name="q_raw%d" % k, align_bytes=64) for k in range(PAIRS)]
+        q_codes = keep.tile([P, PAIRS, 2 * P], U32, name="q_codes", align_bytes=64)
+        q_scales = keep.tile([P, PAIRS, 2 * P], U8, name="q_scales", align_bytes=64)
+        off = [keep.tile([P, S], BF16, name="off%d" % k, align_bytes=64) for k in range(2)]
+        head_scale = [keep.tile([P, 1], BF16, name="head_scale%d" % k) for k in range(2)]
+        row_index = keep.tile([P, 2 * PAIRS, T], I32, name="row_index")
+        token = keep.tile([P, 2 * PAIRS, T], I32, name="token")
+        key_pos = keep.tile([P, 2 * PAIRS, T], F32, name="key_pos")
+        unseen = keep.tile([P, 2 * PAIRS, T], F32, name="unseen")
+        off_masked = keep.tile([P, 2 * PAIRS, T], F32, name="off_masked")
+        yt = keep.tile([P, N_CHUNKS * M * 4], BF16, name="yt", align_bytes=64)
+        y_codes = keep.tile([P, N_CHUNKS * M], U32, name="y_codes", align_bytes=64)
+        y_scales = keep.tile([P, N_CHUNKS * M], U8, name="y_scales", align_bytes=64)
+
+        def load_offsets(group, cols):
+            heads, copies = ((slice(0, 32), 4), (slice(32, 40), 16))[group]
+            shape = [heads.stop - heads.start, copies, cols.stop - cols.start]
+            nc.sync.dma_start(out=off[group][:, cols], in_=offset[heads, cols].unsqueeze(1).to_broadcast(shape))
+
+        def load_scale(group):
+            heads, copies = ((slice(0, 32), 4), (slice(32, 40), 16))[group]
+            shape = [heads.stop - heads.start, copies, 1]
+            with nc.allow_non_contiguous_dma(reason="one head scale for each partition"):
+                nc.sync.dma_start(out=head_scale[group][:], in_=scale[heads].unsqueeze(1).unsqueeze(2).to_broadcast(shape))
+
+        def load_keys(cols):
+            two = slice(2 * cols.start, 2 * cols.stop)
+            nc.sync.dma_start(out=k_codes[:, two].bitcast(I32), in_=keys_words[0][:, two].bitcast(I32))
+
+        first = slice(CHUNK_ORDER[0] * CHUNK, S)
+        rest = slice(0, CHUNK_ORDER[0] * CHUNK)
+        nc.vector.memset(k_scales[:].bitcast(I32), 0)
+        nc.vector.memset(warm[:], 0.0)
+        nc.scalar.activation(out=warm_out[:], in_=warm[:], func=ACT.Sigmoid)
+        nc.sync.dma_start(out=q_raw[0][:], in_=pair_rows(q_rows, 0))
+        load_keys(first)
+        load_offsets(0, first)
+        load_scale(0)
+        for quad in range(4):
+            nc.sync.dma_start(
+                out=k_scales[32 * quad : 32 * quad + 4, :].bitcast(I32),
+                in_=keys_scales[0][4 * quad : 4 * quad + 4, :].bitcast(I32),
+            )
+        nc.sync.dma_start(out=q_raw[1][:], in_=pair_rows(q_rows, 1))
+        load_offsets(1, first)
+        for k in range(2, PAIRS):
+            nc.sync.dma_start(out=q_raw[k][:], in_=pair_rows(q_rows, k))
+        load_scale(1)
+        load_keys(rest)
+        load_offsets(0, rest)
+        load_offsets(1, rest)
+
+        make_identity(nc, ident[:])
+        nc.gpsimd.iota(row_index[:, 0:8, :], pattern=[[1, 8], [0, T]], base=0, channel_multiplier=8)
+        nc.gpsimd.iota(row_index[:, 8:10, :], pattern=[[1, 2], [0, T]], base=0, channel_multiplier=2)
+        nc.gpsimd.iota(key_pos[:], pattern=[[0, 2 * PAIRS], [1, T]], base=0, channel_multiplier=0,
+                       allow_small_or_imprecise_dtypes=True)
+        nc.vector.tensor_scalar(out=token[:], in0=row_index[:], scalar1=T - 1, scalar2=None, op0=ALU.bitwise_and)
+        nc.vector.tensor_tensor(out=unseen[:], in0=token[:], in1=key_pos[:], op=ALU.is_lt)
+
+        def mask_offsets():
+            for group, tiles in enumerate((slice(0, 8), slice(8, 10))):
+                n = tiles.stop - tiles.start
+                nc.vector.scalar_tensor_tensor(
+                    out=off_masked[:, tiles, :], in0=unseen[:, tiles, :], scalar=MASKED,
+                    in1=off[group][:, S - T : S].unsqueeze(1).to_broadcast([P, n, T]),
+                    op0=ALU.mult, op1=ALU.add,
+                )
+
+        q_grouped = {}
+
+        def turn_q(pair):
+            words = q_raw[pair][:].bitcast(F32)
+            bank = psum.tile([P, 2, 2, P], F32, name="turn_bank", tag="turn", bufs=3)
+            for c in range(2):
+                for u in range(2):
+                    nc.tensor.transpose(bank[:, c, u, :], words[:, c, u : D // 2 : 2], ident[:])
+            grouped = work.tile([P, 2 * P * 4], BF16, name="q_grouped", tag="q_grouped", bufs=2, align_bytes=64)
+            copy = nc.vector.tensor_copy if pair == 0 else nc.scalar.copy
+            copy(
+                out=grouped[:].bitcast(F32).rearrange("p (c r u) -> p c r u", c=2, u=2),
+                in_=bank[:].rearrange("p c u r -> p c r u"),
+            )
+            q_grouped[pair] = grouped
+
+        def quantize_q(pair):
+            nc.vector.quantize_mx(out=q_codes[:, pair, :].bitcast(FP8X4), scales=q_scales[:, pair, :],
+                                  in_=q_grouped[pair][:])
+
+        banks, z_of, y_of, yb_of, turned = {}, {}, {}, {}, {}
+
+        def scores(step):
+            pair, g = STEP_PLAN[step][0], CHUNK_ORDER[STEP_PLAN[step][1]]
+            for c in range(2):
+                bank = psum.tile([P, CHUNK], F32, name="score_bank", tag="score", bufs=5)
+                nc.tensor.matmul_mx(
+                    out=bank[:],
+                    lhsT=q_codes[:, pair, c * P : (c + 1) * P].bitcast(FP8X4),
+                    lhsT_scale=q_scales[:, pair, c * P : (c + 1) * P],
+                    rhs=k_codes[:, 2 * g * CHUNK : 2 * (g + 1) * CHUNK].bitcast(FP4X4),
+                    rhs_scale=k_scales[:, g * CHUNK : (g + 1) * CHUNK],
+                    start=True,
+                    stop=True,
+                )
+                banks[step, c] = bank
+
+        def affine(step):
+            pair, g = STEP_PLAN[step][0], CHUNK_ORDER[STEP_PLAN[step][1]]
+            group = pair // (PAIRS - 1)
+            z = work.tile([P, 2, CHUNK], F32, name="z", tag="z", bufs=5)
+            plain = CHUNK - T if g == N_CHUNKS - 1 else CHUNK
+            for c in range(2):
+                nc.vector.scalar_tensor_tensor(
+                    out=z[:, c, 0:plain], in0=banks[step, c][:, 0:plain], scalar=head_scale[group][:],
+                    in1=off[group][:, g * CHUNK : g * CHUNK + plain], op0=ALU.mult, op1=ALU.add,
+                )
+                if plain < CHUNK:
+                    nc.vector.scalar_tensor_tensor(
+                        out=z[:, c, plain:CHUNK], in0=banks[step, c][:, plain:CHUNK],
+                        scalar=head_scale[group][:],
+                        in1=off_masked[:, 2 * pair + c, :], op0=ALU.mult, op1=ALU.add,
+                    )
+            z_of[step] = z
+
+        def sigmoid(step):
+            pair, g = STEP_PLAN[step][0], CHUNK_ORDER[STEP_PLAN[step][1]]
+            y = work.tile([P, 2, CHUNK], F32, name="y", tag="y", bufs=6)
+            nc.scalar.activation(out=y[:], in_=z_of[step][:], func=ACT.Sigmoid)
+            nc.sync.dma_start(out=pair_rows(y_rows, pair)[:, :, g * CHUNK : (g + 1) * CHUNK], in_=y[:])
+            y_of[step] = y
+
+        def round_y(step):
+            yb = work.tile([P, 2, 2 * P, 2], BF16, name="yb", tag="yb", bufs=4, align_bytes=64)
+            src = y_of[step][:].rearrange("p c (r u e) -> p u (c r) e", u=2, e=2)
+            if step in VECTOR_CAST:
+                nc.vector.tensor_copy(out=yb[:], in_=src)
+            else:
+                nc.gpsimd.tensor_scalar(out=yb[:], in0=src, scalar1=1.0, scalar2=0.0, op0=ALU.mult, op1=ALU.add)
+            yb_of[step] = yb
+
+        def turn_y(step):
+            words = yb_of[step][:].rearrange("p u r e -> p u (r e)").bitcast(F32)
+            bank = psum.tile([P, 2, 2, P], F32, name="turn_bank", tag="turn", bufs=3)
+            for c in range(2):
+                for u in range(2):
+                    nc.tensor.transpose(bank[:, c, u, :], words[:, u, c * P : (c + 1) * P], ident[:])
+            turned[step] = bank
+
+        def copy_y(step):
+            pair, pos = STEP_PLAN[step]
+            bank = turned[step]
+            dst = yt[:].bitcast(F32)[:, 2 * pos * M : 2 * (pos + 1) * M]
+            if pair < PAIRS - 1:
+                dst = dst[:, 0 : 2 * M_WIDE].rearrange("p (r w) -> p r w", w=16)[:, :, 4 * pair : 4 * pair + 4]
+            else:
+                dst = dst[:, 2 * M_WIDE : 2 * M].rearrange("p (r w) -> p r w", w=4)
+            src = bank[:].rearrange("p c u r -> p r (c u)")
+            if step in VECTOR_EVAC:
+                nc.vector.tensor_copy(out=dst, in_=src)
+            else:
+                nc.scalar.copy(out=dst, in_=src)
+
+        def quantize_y(col, n):
+            nc.vector.quantize_mx(out=y_codes[:, col : col + n].bitcast(FP8X4), scales=y_scales[:, col : col + n],
+                                  in_=yt[:, 4 * col : 4 * (col + n)])
+
+        def store_planes(col, n):
+            lo = col
+            while lo < col + n:
+                pos = lo // M
+                hi = min(col + n, (pos + 1) * M)
+                dst = out_1[CHUNK_ORDER[pos]].rearrange("p m t -> p (m t)").bitcast(I32)
+                nc.sync.dma_start(out=dst[:, lo - pos * M : hi - pos * M], in_=y_codes[:, lo:hi].bitcast(I32))
+                lo = hi
+            p1 = (col + n) // (2 * M) * 2
+            if p1 > col // (2 * M) * 2:
+                p0 = p1 - 2
+                g0 = CHUNK_ORDER[p0]
+                for quad in range(4):
+                    queue = nc.scalar if (p1 == N_CHUNKS and quad % 2) else nc.sync
+                    queue.dma_start(
+                        out=out_2[g0 : g0 + p1 - p0, 4 * quad : 4 * quad + 4, :].rearrange("g r m -> r g m").bitcast(I32),
+                        in_=y_scales[32 * quad : 32 * quad + 4, p0 * M : p1 * M].bitcast(I32).rearrange(
+                            "r (g m) -> r g m", g=p1 - p0),
+                    )
+
+        turn_q(0)
+        quantize_q(0)
+        turn_q(1)
+        scores(0)
+        scores(1)
+        quantize_q(1)
+        for it in range(STEPS + QUANT_LAG):
+            if it < STEPS:
+                affine(it)
+            if it == 0:
+                mask_offsets()
+            if it in (1, 3, 5):
+                quantize_q(2 + it // 2)
+            if it - VECTOR_COPY_LAG in VECTOR_EVAC:
+                copy_y(it - VECTOR_COPY_LAG)
+            if it - VECTOR_ROUND_LAG in VECTOR_CAST:
+                round_y(it - VECTOR_ROUND_LAG)
+            for last, col, n in WINDOWS:
+                if last + QUANT_LAG == it:
+                    quantize_y(col, n)
+                    store_planes(col, n)
+            if it + SCORE_LEAD < STEPS:
+                scores(it + SCORE_LEAD)
+            if it + 2 < PAIRS:
+                turn_q(it + 2)
+            if it < STEPS:
+                sigmoid(it)
+                if it not in VECTOR_CAST:
+                    round_y(it)
+            if 0 <= it - TURN_LAG < STEPS:
+                turn_y(it - TURN_LAG)
+            if 0 <= it - SCALAR_COPY_LAG < STEPS and it - SCALAR_COPY_LAG not in VECTOR_EVAC:
+                copy_y(it - SCALAR_COPY_LAG)

@@ -20,28 +20,43 @@ ACT = mybir.ActivationFunctionType
 P = 128
 CHUNK = 512
 N_CHUNKS = S // CHUNK
-PAIRS = 5
+TILES = M // P
+PAIRS = TILES // 2
 STEPS = N_CHUNKS * PAIRS
+WIDE_STEPS = 2 * TILES
 M_WIDE = 1024
+WIDE_TILES = 8
+GROUPS = ((slice(0, 32), 4), (slice(32, 40), 16))
 CHUNK_ORDER = [4, 5, 0, 1, 2, 3]
-STEP_PLAN = [(s // 2, s % 2) for s in range(2 * PAIRS)] + [(s % PAIRS, s // PAIRS) for s in range(2 * PAIRS, STEPS)]
 MASKED = -(2.0 ** 126)
-SCORE_LEAD = 2
-TURN_LAG = 3
-SCALAR_COPY_LAG = 4
-VECTOR_COPY_LAG = 5
-VECTOR_ROUND_LAG = 3
-QUANT_LAG = 8
-VECTOR_EVAC = range(1, 24, 4)
-VECTOR_CAST = range(STEPS - 3, STEPS)
-WINDOWS = [(6, 0, 1024), (8, 1024, 1024), (13, 2048, 1024), (18, 3072, 1024), (19, 4096, 1024),
-           (23, 5120, 1024), (24, 6144, 256), (28, 6400, 1024), (29, 7424, 256)]
+WINDOWS = [(0, 1024), (1024, 1024), (2048, 1024), (3072, 1024), (4096, 1024),
+           (5120, 1024), (6144, 256), (6400, 1024), (7424, 256)]
+QUANT_AT = [17,22,31,31,33,39,41,41,44]
+VECTOR_COPIES = [3,5,10,15,17,19,20]
+VECTOR_ROUNDS = [6,11,17,20,27,28,29]
+VECTOR_Q_COPIES = []
+Q_QUANT_LEAD, Q_TURN_LEAD, SCORE_LEAD = 2, 3, 1
+SIGMOID_LAG, VECTOR_ROUND_LAG, TURN_LAG, SCALAR_COPY_LAG, VECTOR_COPY_LAG = 1, 2, 7, 8, 9
 
 
-def pair_rows(rows, pair):
-    if pair < PAIRS - 1:
-        return rows[0:M_WIDE, :].rearrange("(p c) n -> p c n", c=8)[:, 2 * pair : 2 * pair + 2, :]
-    return rows[M_WIDE:M, :].rearrange("(p c) n -> p c n", c=2)
+def step_items(step):
+    if step < WIDE_STEPS:
+        return [(step % TILES, 2 * (step // TILES) + i) for i in range(2)]
+    pos, pair = divmod(step, PAIRS)
+    return [(2 * pair + i, pos) for i in range(2)]
+
+
+def bank_order():
+    order = []
+    for step in range(STEPS):
+        order.extend((pos, tile // 2) for tile, pos in step_items(step) if tile % 2)
+    return order
+
+
+def group_rows(rows, group):
+    if group == 0:
+        return rows[0:M_WIDE, :].rearrange("(p c) n -> p c n", c=WIDE_TILES)
+    return rows[M_WIDE:M, :].rearrange("(p c) n -> p c n", c=TILES - WIDE_TILES)
 
 
 def tile_causal_sigmoid_attention_weights_g4_kernel(
@@ -50,6 +65,7 @@ def tile_causal_sigmoid_attention_weights_g4_kernel(
     nc = tc.nc
     q_rows = q.rearrange("h i d -> (h i) d")
     y_rows = out_0.rearrange("h i j -> (h i) j")
+    banks_in_order = bank_order()
 
     with ExitStack() as ctx:
         keep = ctx.enter_context(tc.tile_pool(name="keep", bufs=1))
@@ -62,27 +78,32 @@ def tile_causal_sigmoid_attention_weights_g4_kernel(
         warm_out = keep.tile([P, 1], F32, name="warm_out")
         k_codes = keep.tile([P, 2 * S], U8, name="k_codes", align_bytes=64)
         k_scales = keep.tile([P, S], U8, name="k_scales", align_bytes=64)
-        q_raw = [keep.tile([P, 2, D], BF16, name="q_raw%d" % k, align_bytes=64) for k in range(PAIRS)]
-        q_codes = keep.tile([P, PAIRS, 2 * P], U32, name="q_codes", align_bytes=64)
-        q_scales = keep.tile([P, PAIRS, 2 * P], U8, name="q_scales", align_bytes=64)
+        q_raw = keep.tile([P, TILES, D], BF16, name="q_raw", align_bytes=64)
+        q_codes = keep.tile([P, TILES, P], U32, name="q_codes", align_bytes=64)
+        q_scales = keep.tile([P, TILES, P], U8, name="q_scales", align_bytes=64)
         off = [keep.tile([P, S], BF16, name="off%d" % k, align_bytes=64) for k in range(2)]
         head_scale = [keep.tile([P, 1], BF16, name="head_scale%d" % k) for k in range(2)]
-        row_index = keep.tile([P, 2 * PAIRS, T], I32, name="row_index")
-        token = keep.tile([P, 2 * PAIRS, T], I32, name="token")
-        key_pos = keep.tile([P, 2 * PAIRS, T], F32, name="key_pos")
-        unseen = keep.tile([P, 2 * PAIRS, T], F32, name="unseen")
-        off_masked = keep.tile([P, 2 * PAIRS, T], F32, name="off_masked")
+        row_index = keep.tile([P, TILES, T], I32, name="row_index")
+        token = keep.tile([P, TILES, T], I32, name="token")
+        key_pos = keep.tile([P, TILES, T], F32, name="key_pos")
+        unseen = keep.tile([P, TILES, T], F32, name="unseen")
+        off_masked = keep.tile([P, TILES, T], F32, name="off_masked")
         yt = keep.tile([P, N_CHUNKS * M * 4], BF16, name="yt", align_bytes=64)
         y_codes = keep.tile([P, N_CHUNKS * M], U32, name="y_codes", align_bytes=64)
         y_scales = keep.tile([P, N_CHUNKS * M], U8, name="y_scales", align_bytes=64)
 
+        def load_q(lo, hi):
+            group = lo // WIDE_TILES
+            base = group * WIDE_TILES
+            nc.sync.dma_start(out=q_raw[:, lo:hi, :], in_=group_rows(q_rows, group)[:, lo - base : hi - base, :])
+
         def load_offsets(group, cols):
-            heads, copies = ((slice(0, 32), 4), (slice(32, 40), 16))[group]
+            heads, copies = GROUPS[group]
             shape = [heads.stop - heads.start, copies, cols.stop - cols.start]
             nc.sync.dma_start(out=off[group][:, cols], in_=offset[heads, cols].unsqueeze(1).to_broadcast(shape))
 
         def load_scale(group):
-            heads, copies = ((slice(0, 32), 4), (slice(32, 40), 16))[group]
+            heads, copies = GROUPS[group]
             shape = [heads.stop - heads.start, copies, 1]
             with nc.allow_non_contiguous_dma(reason="one head scale for each partition"):
                 nc.sync.dma_start(out=head_scale[group][:], in_=scale[heads].unsqueeze(1).unsqueeze(2).to_broadcast(shape))
@@ -90,25 +111,25 @@ def tile_causal_sigmoid_attention_weights_g4_kernel(
         def load_keys(cols):
             two = slice(2 * cols.start, 2 * cols.stop)
             nc.sync.dma_start(out=k_codes[:, two].bitcast(I32), in_=keys_words[0][:, two].bitcast(I32))
+            for quad in range(4):
+                rows = keys_scales[0][4 * quad : 4 * quad + 4, cols].bitcast(I32)
+                nc.sync.dma_start(
+                    out=k_scales[32 * quad : 32 * quad + 32, cols].bitcast(I32),
+                    in_=rows.unsqueeze(0).to_broadcast([8, 4, (cols.stop - cols.start) // 4]),
+                )
 
         first = slice(CHUNK_ORDER[0] * CHUNK, S)
         rest = slice(0, CHUNK_ORDER[0] * CHUNK)
-        nc.vector.memset(k_scales[:].bitcast(I32), 0)
         nc.vector.memset(warm[:], 0.0)
         nc.scalar.activation(out=warm_out[:], in_=warm[:], func=ACT.Sigmoid)
-        nc.sync.dma_start(out=q_raw[0][:], in_=pair_rows(q_rows, 0))
+        load_q(0, 2)
         load_keys(first)
         load_offsets(0, first)
         load_scale(0)
-        for quad in range(4):
-            nc.sync.dma_start(
-                out=k_scales[32 * quad : 32 * quad + 4, :].bitcast(I32),
-                in_=keys_scales[0][4 * quad : 4 * quad + 4, :].bitcast(I32),
-            )
-        nc.sync.dma_start(out=q_raw[1][:], in_=pair_rows(q_rows, 1))
+        load_q(2, 4)
         load_offsets(1, first)
-        for k in range(2, PAIRS):
-            nc.sync.dma_start(out=q_raw[k][:], in_=pair_rows(q_rows, k))
+        load_q(4, 8)
+        load_q(8, 10)
         load_scale(1)
         load_keys(rest)
         load_offsets(0, rest)
@@ -117,118 +138,113 @@ def tile_causal_sigmoid_attention_weights_g4_kernel(
         make_identity(nc, ident[:])
         nc.gpsimd.iota(row_index[:, 0:8, :], pattern=[[1, 8], [0, T]], base=0, channel_multiplier=8)
         nc.gpsimd.iota(row_index[:, 8:10, :], pattern=[[1, 2], [0, T]], base=0, channel_multiplier=2)
-        nc.gpsimd.iota(key_pos[:], pattern=[[0, 2 * PAIRS], [1, T]], base=0, channel_multiplier=0,
+        nc.gpsimd.iota(key_pos[:], pattern=[[0, TILES], [1, T]], base=0, channel_multiplier=0,
                        allow_small_or_imprecise_dtypes=True)
         nc.vector.tensor_scalar(out=token[:], in0=row_index[:], scalar1=T - 1, scalar2=None, op0=ALU.bitwise_and)
         nc.vector.tensor_tensor(out=unseen[:], in0=token[:], in1=key_pos[:], op=ALU.is_lt)
 
-        def mask_offsets():
-            for group, tiles in enumerate((slice(0, 8), slice(8, 10))):
-                n = tiles.stop - tiles.start
-                nc.vector.scalar_tensor_tensor(
-                    out=off_masked[:, tiles, :], in0=unseen[:, tiles, :], scalar=MASKED,
-                    in1=off[group][:, S - T : S].unsqueeze(1).to_broadcast([P, n, T]),
-                    op0=ALU.mult, op1=ALU.add,
-                )
-
-        q_grouped = {}
-
-        def turn_q(pair):
-            words = q_raw[pair][:].bitcast(F32)
-            bank = psum.tile([P, 2, 2, P], F32, name="turn_bank", tag="turn", bufs=3)
-            for c in range(2):
-                for u in range(2):
-                    nc.tensor.transpose(bank[:, c, u, :], words[:, c, u : D // 2 : 2], ident[:])
-            grouped = work.tile([P, 2 * P * 4], BF16, name="q_grouped", tag="q_grouped", bufs=2, align_bytes=64)
-            copy = nc.vector.tensor_copy if pair == 0 else nc.scalar.copy
-            copy(
-                out=grouped[:].bitcast(F32).rearrange("p (c r u) -> p c r u", c=2, u=2),
-                in_=bank[:].rearrange("p c u r -> p c r u"),
+        def mask_offsets(group):
+            tiles = (slice(0, WIDE_TILES), slice(WIDE_TILES, TILES))[group]
+            nc.vector.scalar_tensor_tensor(
+                out=off_masked[:, tiles, :], in0=unseen[:, tiles, :], scalar=MASKED,
+                in1=off[group][:, S - T : S].unsqueeze(1).to_broadcast([P, tiles.stop - tiles.start, T]),
+                op0=ALU.mult, op1=ALU.add,
             )
-            q_grouped[pair] = grouped
 
-        def quantize_q(pair):
-            nc.vector.quantize_mx(out=q_codes[:, pair, :].bitcast(FP8X4), scales=q_scales[:, pair, :],
-                                  in_=q_grouped[pair][:])
+        q_grouped, score_banks, z_of, y_of, yb_of, turned = {}, {}, {}, {}, {}, {}
 
-        banks, z_of, y_of, yb_of, turned = {}, {}, {}, {}, {}
+        def turn_q(tile):
+            words = q_raw[:, tile, :].bitcast(F32)
+            bank = psum.tile([P, 2, P], F32, name="q_bank", tag="turn", bufs=4)
+            for u in range(2):
+                nc.tensor.transpose(bank[:, u, :], words[:, u : D // 2 : 2], ident[:])
+            grouped = work.tile([P, 4 * P], BF16, name="q_grouped", tag="q_grouped", bufs=3, align_bytes=64)
+            copy = nc.vector.tensor_copy if tile in VECTOR_Q_COPIES else nc.scalar.copy
+            copy(out=grouped[:].bitcast(F32).rearrange("p (r u) -> p r u", u=2), in_=bank[:].rearrange("p u r -> p r u"))
+            q_grouped[tile] = grouped
+
+        def quantize_q(tile):
+            nc.vector.quantize_mx(out=q_codes[:, tile, :].bitcast(FP8X4), scales=q_scales[:, tile, :],
+                                  in_=q_grouped[tile][:])
 
         def scores(step):
-            pair, g = STEP_PLAN[step][0], CHUNK_ORDER[STEP_PLAN[step][1]]
-            for c in range(2):
-                bank = psum.tile([P, CHUNK], F32, name="score_bank", tag="score", bufs=5)
+            for i, (tile, pos) in enumerate(step_items(step)):
+                g = CHUNK_ORDER[pos]
+                bank = psum.tile([P, CHUNK], F32, name="score_bank", tag="score", bufs=4)
                 nc.tensor.matmul_mx(
                     out=bank[:],
-                    lhsT=q_codes[:, pair, c * P : (c + 1) * P].bitcast(FP8X4),
-                    lhsT_scale=q_scales[:, pair, c * P : (c + 1) * P],
+                    lhsT=q_codes[:, tile, :].bitcast(FP8X4),
+                    lhsT_scale=q_scales[:, tile, :],
                     rhs=k_codes[:, 2 * g * CHUNK : 2 * (g + 1) * CHUNK].bitcast(FP4X4),
                     rhs_scale=k_scales[:, g * CHUNK : (g + 1) * CHUNK],
                     start=True,
                     stop=True,
                 )
-                banks[step, c] = bank
+                score_banks[step, i] = bank
 
         def affine(step):
-            pair, g = STEP_PLAN[step][0], CHUNK_ORDER[STEP_PLAN[step][1]]
-            group = pair // (PAIRS - 1)
-            z = work.tile([P, 2, CHUNK], F32, name="z", tag="z", bufs=5)
-            plain = CHUNK - T if g == N_CHUNKS - 1 else CHUNK
-            for c in range(2):
+            z = work.tile([P, 2, CHUNK], F32, name="z", tag="z", bufs=4)
+            for i, (tile, pos) in enumerate(step_items(step)):
+                g, group = CHUNK_ORDER[pos], tile // WIDE_TILES
+                plain = CHUNK - T if g == N_CHUNKS - 1 else CHUNK
                 nc.vector.scalar_tensor_tensor(
-                    out=z[:, c, 0:plain], in0=banks[step, c][:, 0:plain], scalar=head_scale[group][:],
+                    out=z[:, i, 0:plain], in0=score_banks[step, i][:, 0:plain], scalar=head_scale[group][:],
                     in1=off[group][:, g * CHUNK : g * CHUNK + plain], op0=ALU.mult, op1=ALU.add,
                 )
                 if plain < CHUNK:
                     nc.vector.scalar_tensor_tensor(
-                        out=z[:, c, plain:CHUNK], in0=banks[step, c][:, plain:CHUNK],
-                        scalar=head_scale[group][:],
-                        in1=off_masked[:, 2 * pair + c, :], op0=ALU.mult, op1=ALU.add,
+                        out=z[:, i, plain:CHUNK], in0=score_banks[step, i][:, plain:CHUNK],
+                        scalar=head_scale[group][:], in1=off_masked[:, tile, :], op0=ALU.mult, op1=ALU.add,
                     )
             z_of[step] = z
 
         def sigmoid(step):
-            pair, g = STEP_PLAN[step][0], CHUNK_ORDER[STEP_PLAN[step][1]]
-            y = work.tile([P, 2, CHUNK], F32, name="y", tag="y", bufs=6)
-            nc.scalar.activation(out=y[:], in_=z_of[step][:], func=ACT.Sigmoid)
-            nc.sync.dma_start(out=pair_rows(y_rows, pair)[:, :, g * CHUNK : (g + 1) * CHUNK], in_=y[:])
+            (tile, pos), (last_tile, last_pos) = step_items(step)
+            group = tile // WIDE_TILES
+            base = group * WIDE_TILES
+            keys = slice(CHUNK_ORDER[pos] * CHUNK, (CHUNK_ORDER[last_pos] + 1) * CHUNK)
+            dst = group_rows(y_rows, group)[:, tile - base : last_tile - base + 1, keys]
+            y = work.tile([P, 2 * CHUNK], F32, name="y", tag="y", bufs=6)
+            nc.scalar.activation(out=y[:], in_=z_of[step][:].rearrange("p i n -> p (i n)"), func=ACT.Sigmoid)
+            nc.sync.dma_start(out=dst, in_=y[:].rearrange("p (c n) -> p c n", c=last_tile - tile + 1))
             y_of[step] = y
 
         def round_y(step):
-            yb = work.tile([P, 2, 2 * P, 2], BF16, name="yb", tag="yb", bufs=4, align_bytes=64)
-            src = y_of[step][:].rearrange("p c (r u e) -> p u (c r) e", u=2, e=2)
-            if step in VECTOR_CAST:
-                nc.vector.tensor_copy(out=yb[:], in_=src)
+            yb = work.tile([P, 2 * CHUNK], BF16, name="yb", tag="yb", bufs=6, align_bytes=64)
+            if step in VECTOR_ROUNDS:
+                nc.vector.tensor_copy(out=yb[:].rearrange("p (u r e) -> p u r e", u=2, e=2),
+                                      in_=y_of[step][:].rearrange("p (r u e) -> p u r e", u=2, e=2))
             else:
-                nc.gpsimd.tensor_scalar(out=yb[:], in0=src, scalar1=1.0, scalar2=0.0, op0=ALU.mult, op1=ALU.add)
+                nc.gpsimd.tensor_scalar(out=yb[:], in0=y_of[step][:], scalar1=1.0, scalar2=0.0,
+                                        op0=ALU.mult, op1=ALU.add)
             yb_of[step] = yb
 
         def turn_y(step):
-            words = yb_of[step][:].rearrange("p u r e -> p u (r e)").bitcast(F32)
-            bank = psum.tile([P, 2, 2, P], F32, name="turn_bank", tag="turn", bufs=3)
-            for c in range(2):
+            words = yb_of[step][:].bitcast(F32)
+            for i, (tile, pos) in enumerate(step_items(step)):
+                if tile % 2 == 0:
+                    turned[pos, tile // 2] = psum.tile([P, 2, 2, P], F32, name="y_bank", tag="turn", bufs=4)
+                bank = turned[pos, tile // 2]
                 for u in range(2):
-                    nc.tensor.transpose(bank[:, c, u, :], words[:, u, c * P : (c + 1) * P], ident[:])
-            turned[step] = bank
+                    if step in VECTOR_ROUNDS:
+                        src = words[:, (2 * u + i) * P : (2 * u + i + 1) * P]
+                    else:
+                        src = words[:, 2 * i * P + u : 2 * (i + 1) * P : 2]
+                    nc.tensor.transpose(bank[:, tile % 2, u, :], src, ident[:])
 
-        def copy_y(step):
-            pair, pos = STEP_PLAN[step]
-            bank = turned[step]
+        def copy_y(index):
+            pos, pair = banks_in_order[index]
             dst = yt[:].bitcast(F32)[:, 2 * pos * M : 2 * (pos + 1) * M]
             if pair < PAIRS - 1:
                 dst = dst[:, 0 : 2 * M_WIDE].rearrange("p (r w) -> p r w", w=16)[:, :, 4 * pair : 4 * pair + 4]
             else:
                 dst = dst[:, 2 * M_WIDE : 2 * M].rearrange("p (r w) -> p r w", w=4)
-            src = bank[:].rearrange("p c u r -> p r (c u)")
-            if step in VECTOR_EVAC:
-                nc.vector.tensor_copy(out=dst, in_=src)
-            else:
-                nc.scalar.copy(out=dst, in_=src)
+            copy = nc.vector.tensor_copy if index in VECTOR_COPIES else nc.scalar.copy
+            copy(out=dst, in_=turned[pos, pair][:].rearrange("p c u r -> p r (c u)"))
 
         def quantize_y(col, n):
             nc.vector.quantize_mx(out=y_codes[:, col : col + n].bitcast(FP8X4), scales=y_scales[:, col : col + n],
                                   in_=yt[:, 4 * col : 4 * (col + n)])
-
-        def store_planes(col, n):
             lo = col
             while lo < col + n:
                 pos = lo // M
@@ -243,41 +259,43 @@ def tile_causal_sigmoid_attention_weights_g4_kernel(
                 for quad in range(4):
                     queue = nc.scalar if (p1 == N_CHUNKS and quad % 2) else nc.sync
                     queue.dma_start(
-                        out=out_2[g0 : g0 + p1 - p0, 4 * quad : 4 * quad + 4, :].rearrange("g r m -> r g m").bitcast(I32),
+                        out=out_2[g0 : g0 + 2, 4 * quad : 4 * quad + 4, :].rearrange("g r m -> r g m").bitcast(I32),
                         in_=y_scales[32 * quad : 32 * quad + 4, p0 * M : p1 * M].bitcast(I32).rearrange(
-                            "r (g m) -> r g m", g=p1 - p0),
+                            "r (g m) -> r g m", g=2),
                     )
 
         turn_q(0)
-        quantize_q(0)
         turn_q(1)
+        quantize_q(0)
         scores(0)
-        scores(1)
-        quantize_q(1)
-        for it in range(STEPS + QUANT_LAG):
-            if it < STEPS:
-                affine(it)
+        for it in range(-1, max(QUANT_AT) + 1):
             if it == 0:
-                mask_offsets()
-            if it in (1, 3, 5):
-                quantize_q(2 + it // 2)
-            if it - VECTOR_COPY_LAG in VECTOR_EVAC:
+                mask_offsets(0)
+            if 0 <= it < STEPS:
+                affine(it)
+            if it == 1:
+                mask_offsets(1)
+            if 1 <= it + Q_QUANT_LEAD < TILES:
+                quantize_q(it + Q_QUANT_LEAD)
+            if it - VECTOR_COPY_LAG in VECTOR_COPIES:
                 copy_y(it - VECTOR_COPY_LAG)
-            if it - VECTOR_ROUND_LAG in VECTOR_CAST:
-                round_y(it - VECTOR_ROUND_LAG)
-            for last, col, n in WINDOWS:
-                if last + QUANT_LAG == it:
+            for at, (col, n) in zip(QUANT_AT, WINDOWS):
+                if at == it:
                     quantize_y(col, n)
-                    store_planes(col, n)
-            if it + SCORE_LEAD < STEPS:
+            if it - VECTOR_ROUND_LAG in VECTOR_ROUNDS:
+                round_y(it - VECTOR_ROUND_LAG)
+            if 1 <= it + SCORE_LEAD < STEPS:
                 scores(it + SCORE_LEAD)
-            if it + 2 < PAIRS:
-                turn_q(it + 2)
-            if it < STEPS:
-                sigmoid(it)
-                if it not in VECTOR_CAST:
-                    round_y(it)
-            if 0 <= it - TURN_LAG < STEPS:
-                turn_y(it - TURN_LAG)
-            if 0 <= it - SCALAR_COPY_LAG < STEPS and it - SCALAR_COPY_LAG not in VECTOR_EVAC:
-                copy_y(it - SCALAR_COPY_LAG)
+            if 2 <= it + Q_TURN_LEAD < TILES:
+                turn_q(it + Q_TURN_LEAD)
+            step = it - SIGMOID_LAG
+            if 0 <= step < STEPS:
+                sigmoid(step)
+                if step not in VECTOR_ROUNDS:
+                    round_y(step)
+            step = it - TURN_LAG
+            if 0 <= step < STEPS:
+                turn_y(step)
+            index = it - SCALAR_COPY_LAG
+            if 0 <= index < STEPS and index not in VECTOR_COPIES:
+                copy_y(index)

@@ -31,12 +31,14 @@ CHUNK_ORDER = [4, 5, 0, 1, 2, 3]
 MASKED = -(2.0 ** 126)
 WINDOWS = [(0, 1024), (1024, 1024), (2048, 1024), (3072, 1024), (4096, 1024),
            (5120, 1024), (6144, 256), (6400, 1024), (7424, 256)]
-QUANT_AT = [17,22,31,31,33,39,41,41,44]
-VECTOR_COPIES = [3,5,10,15,17,19,20]
-VECTOR_ROUNDS = [6,11,17,20,27,28,29]
-VECTOR_Q_COPIES = []
-Q_QUANT_LEAD, Q_TURN_LEAD, SCORE_LEAD = 2, 3, 1
-SIGMOID_LAG, VECTOR_ROUND_LAG, TURN_LAG, SCALAR_COPY_LAG, VECTOR_COPY_LAG = 1, 2, 7, 8, 9
+QUANT_AT = [14,20,24,29,30,30,33,34,35]
+VECTOR_COPIES = []
+VECTOR_ROUNDS = [0,2,4,6,8,10,12,14,16,18,20,22,24,27,28,29]
+VECTOR_Q_COPIES = [0]
+Q_QUANT_AT = {-1: 1, 0: 2, 2: 4, 4: 6, 6: 8}
+Q_TURN_AT = {-1: 2, 1: 4, 2: 6, 3: 8}
+SCORE_LEAD = 1
+SIGMOID_LAG, VECTOR_ROUND_LAG, TURN_LAG, SCALAR_COPY_LAG, VECTOR_COPY_LAG = 0, 2, 4, 5, 8
 
 
 def step_items(step):
@@ -79,8 +81,8 @@ def tile_causal_sigmoid_attention_weights_g4_kernel(
         k_codes = keep.tile([P, 2 * S], U8, name="k_codes", align_bytes=64)
         k_scales = keep.tile([P, S], U8, name="k_scales", align_bytes=64)
         q_raw = keep.tile([P, TILES, D], BF16, name="q_raw", align_bytes=64)
-        q_codes = keep.tile([P, TILES, P], U32, name="q_codes", align_bytes=64)
-        q_scales = keep.tile([P, TILES, P], U8, name="q_scales", align_bytes=64)
+        q_codes = keep.tile([P, M], U32, name="q_codes", align_bytes=64)
+        q_scales = keep.tile([P, M], U8, name="q_scales", align_bytes=64)
         off = [keep.tile([P, S], BF16, name="off%d" % k, align_bytes=64) for k in range(2)]
         head_scale = [keep.tile([P, 1], BF16, name="head_scale%d" % k) for k in range(2)]
         row_index = keep.tile([P, TILES, T], I32, name="row_index")
@@ -153,19 +155,23 @@ def tile_causal_sigmoid_attention_weights_g4_kernel(
 
         q_grouped, score_banks, z_of, y_of, yb_of, turned = {}, {}, {}, {}, {}, {}
 
-        def turn_q(tile):
-            words = q_raw[:, tile, :].bitcast(F32)
-            bank = psum.tile([P, 2, P], F32, name="q_bank", tag="turn", bufs=4)
-            for u in range(2):
-                nc.tensor.transpose(bank[:, u, :], words[:, u : D // 2 : 2], ident[:])
-            grouped = work.tile([P, 4 * P], BF16, name="q_grouped", tag="q_grouped", bufs=3, align_bytes=64)
-            copy = nc.vector.tensor_copy if tile in VECTOR_Q_COPIES else nc.scalar.copy
-            copy(out=grouped[:].bitcast(F32).rearrange("p (r u) -> p r u", u=2), in_=bank[:].rearrange("p u r -> p r u"))
-            q_grouped[tile] = grouped
+        def turn_q(lo):
+            n = 1 if lo < 2 else 2
+            bank = psum.tile([P, n, 2, P], F32, name="q_bank", tag="turn", bufs=4)
+            for c in range(n):
+                words = q_raw[:, lo + c, :].bitcast(F32)
+                for u in range(2):
+                    nc.tensor.transpose(bank[:, c, u, :], words[:, u : D // 2 : 2], ident[:])
+            grouped = work.tile([P, n * 4 * P], BF16, name="q_grouped", tag="q_grouped", bufs=3, align_bytes=64)
+            copy = nc.vector.tensor_copy if lo == 0 else nc.scalar.copy
+            copy(out=grouped[:].bitcast(F32).rearrange("p (c r u) -> p c r u", c=n, u=2),
+                 in_=bank[:].rearrange("p c u r -> p c r u"))
+            q_grouped[lo] = grouped
 
-        def quantize_q(tile):
-            nc.vector.quantize_mx(out=q_codes[:, tile, :].bitcast(FP8X4), scales=q_scales[:, tile, :],
-                                  in_=q_grouped[tile][:])
+        def quantize_q(lo):
+            n = 1 if lo < 2 else 2
+            nc.vector.quantize_mx(out=q_codes[:, lo * P : (lo + n) * P].bitcast(FP8X4),
+                                  scales=q_scales[:, lo * P : (lo + n) * P], in_=q_grouped[lo][:])
 
         def scores(step):
             for i, (tile, pos) in enumerate(step_items(step)):
@@ -173,8 +179,8 @@ def tile_causal_sigmoid_attention_weights_g4_kernel(
                 bank = psum.tile([P, CHUNK], F32, name="score_bank", tag="score", bufs=4)
                 nc.tensor.matmul_mx(
                     out=bank[:],
-                    lhsT=q_codes[:, tile, :].bitcast(FP8X4),
-                    lhsT_scale=q_scales[:, tile, :],
+                    lhsT=q_codes[:, tile * P : (tile + 1) * P].bitcast(FP8X4),
+                    lhsT_scale=q_scales[:, tile * P : (tile + 1) * P],
                     rhs=k_codes[:, 2 * g * CHUNK : 2 * (g + 1) * CHUNK].bitcast(FP4X4),
                     rhs_scale=k_scales[:, g * CHUNK : (g + 1) * CHUNK],
                     start=True,
@@ -183,7 +189,7 @@ def tile_causal_sigmoid_attention_weights_g4_kernel(
                 score_banks[step, i] = bank
 
         def affine(step):
-            z = work.tile([P, 2, CHUNK], F32, name="z", tag="z", bufs=4)
+            z = work.tile([P, 2, CHUNK], F32, name="z", tag="z", bufs=5)
             for i, (tile, pos) in enumerate(step_items(step)):
                 g, group = CHUNK_ORDER[pos], tile // WIDE_TILES
                 plain = CHUNK - T if g == N_CHUNKS - 1 else CHUNK
@@ -275,26 +281,29 @@ def tile_causal_sigmoid_attention_weights_g4_kernel(
                 affine(it)
             if it == 1:
                 mask_offsets(1)
-            if 1 <= it + Q_QUANT_LEAD < TILES:
-                quantize_q(it + Q_QUANT_LEAD)
+            if it in Q_QUANT_AT:
+                quantize_q(Q_QUANT_AT[it])
             if it - VECTOR_COPY_LAG in VECTOR_COPIES:
                 copy_y(it - VECTOR_COPY_LAG)
+            if it - VECTOR_ROUND_LAG in VECTOR_ROUNDS:
+                round_y(it - VECTOR_ROUND_LAG)
             for at, (col, n) in zip(QUANT_AT, WINDOWS):
                 if at == it:
                     quantize_y(col, n)
-            if it - VECTOR_ROUND_LAG in VECTOR_ROUNDS:
-                round_y(it - VECTOR_ROUND_LAG)
             if 1 <= it + SCORE_LEAD < STEPS:
                 scores(it + SCORE_LEAD)
-            if 2 <= it + Q_TURN_LEAD < TILES:
-                turn_q(it + Q_TURN_LEAD)
+            if it in Q_TURN_AT:
+                turn_q(Q_TURN_AT[it])
             step = it - SIGMOID_LAG
             if 0 <= step < STEPS:
                 sigmoid(step)
                 if step not in VECTOR_ROUNDS:
                     round_y(step)
             step = it - TURN_LAG
-            if 0 <= step < STEPS:
+            if WIDE_STEPS <= step < STEPS:
+                turn_y(step)
+            elif 0 <= step < WIDE_STEPS and step % 2:
+                turn_y(step - 1)
                 turn_y(step)
             index = it - SCALAR_COPY_LAG
             if 0 <= index < STEPS and index not in VECTOR_COPIES:

@@ -20,39 +20,25 @@ ACT = mybir.ActivationFunctionType
 P = 128
 CHUNK = 512
 N_CHUNKS = S // CHUNK
+SPAN = 2 * CHUNK
 TILES = M // P
-PAIRS = TILES // 2
-STEPS = N_CHUNKS * PAIRS
-WIDE_STEPS = 2 * TILES
-M_WIDE = 1024
 WIDE_TILES = 8
+M_WIDE = WIDE_TILES * P
+STEPS = TILES * S // SPAN
 GROUPS = ((slice(0, 32), 4), (slice(32, 40), 16))
-CHUNK_ORDER = [4, 5, 0, 1, 2, 3]
-MASKED = -(2.0 ** 126)
-WINDOWS = [(0, 1024), (1024, 1024), (2048, 1024), (3072, 1024), (4096, 1024),
-           (5120, 1024), (6144, 256), (6400, 1024), (7424, 256)]
-QUANT_AT = [14,20,24,29,30,30,33,34,35]
-VECTOR_COPIES = []
-VECTOR_ROUNDS = [0,2,4,6,8,10,12,14,16,18,20,22,24,27,28,29]
-VECTOR_Q_COPIES = [0]
-Q_QUANT_AT = {-1: 1, 0: 2, 2: 4, 4: 6, 6: 8}
-Q_TURN_AT = {-1: 2, 1: 4, 2: 6, 3: 8}
+SWEEP_CHUNK = (4, 0, 2)
+MASKED = -(2.0**126)
+
 SCORE_LEAD = 1
-SIGMOID_LAG, VECTOR_ROUND_LAG, TURN_LAG, SCALAR_COPY_LAG, VECTOR_COPY_LAG = 0, 2, 4, 5, 8
-
-
-def step_items(step):
-    if step < WIDE_STEPS:
-        return [(step % TILES, 2 * (step // TILES) + i) for i in range(2)]
-    pos, pair = divmod(step, PAIRS)
-    return [(2 * pair + i, pos) for i in range(2)]
-
-
-def bank_order():
-    order = []
-    for step in range(STEPS):
-        order.extend((pos, tile // 2) for tile, pos in step_items(step) if tile % 2)
-    return order
+VECTOR_ROUND_LAG = 2
+TURN_LAG = 3
+SCALAR_COPY_LAG = 4
+VECTOR_COPY_LAG = 6
+QUANT_LAG = 12
+LAST_QUANT = 33
+PAIRED_TURNS = 26
+VECTOR_ROUNDS = (2, 10, 20, 27, 28, 29)
+VECTOR_COPIES = (2, 12, 22, 25)
 
 
 def group_rows(rows, group):
@@ -67,7 +53,7 @@ def tile_causal_sigmoid_attention_weights_g4_kernel(
     nc = tc.nc
     q_rows = q.rearrange("h i d -> (h i) d")
     y_rows = out_0.rearrange("h i j -> (h i) j")
-    banks_in_order = bank_order()
+    code_words = out_1.rearrange("g p m t -> p g (m t)").bitcast(I32)
 
     with ExitStack() as ctx:
         keep = ctx.enter_context(tc.tile_pool(name="keep", bufs=1))
@@ -76,28 +62,38 @@ def tile_causal_sigmoid_attention_weights_g4_kernel(
         ctx.enter_context(tc.manual_schedule())
 
         ident = keep.tile([P, P], F32, name="ident")
-        warm = keep.tile([P, 1], F32, name="warm")
+        warm_in = keep.tile([P, 1], F32, name="warm_in")
         warm_out = keep.tile([P, 1], F32, name="warm_out")
         k_codes = keep.tile([P, 2 * S], U8, name="k_codes", align_bytes=64)
         k_scales = keep.tile([P, S], U8, name="k_scales", align_bytes=64)
         q_raw = keep.tile([P, TILES, D], BF16, name="q_raw", align_bytes=64)
         q_codes = keep.tile([P, M], U32, name="q_codes", align_bytes=64)
         q_scales = keep.tile([P, M], U8, name="q_scales", align_bytes=64)
-        off = [keep.tile([P, S], BF16, name="off%d" % k, align_bytes=64) for k in range(2)]
-        head_scale = [keep.tile([P, 1], BF16, name="head_scale%d" % k) for k in range(2)]
+        off = [keep.tile([P, S], BF16, name="off%d" % group, align_bytes=64) for group in range(2)]
+        head_scale = [keep.tile([P, 1], BF16, name="head_scale%d" % group) for group in range(2)]
         row_index = keep.tile([P, TILES, T], I32, name="row_index")
         token = keep.tile([P, TILES, T], I32, name="token")
         key_pos = keep.tile([P, TILES, T], F32, name="key_pos")
         unseen = keep.tile([P, TILES, T], F32, name="unseen")
         off_masked = keep.tile([P, TILES, T], F32, name="off_masked")
-        yt = keep.tile([P, N_CHUNKS * M * 4], BF16, name="yt", align_bytes=64)
-        y_codes = keep.tile([P, N_CHUNKS * M], U32, name="y_codes", align_bytes=64)
-        y_scales = keep.tile([P, N_CHUNKS * M], U8, name="y_scales", align_bytes=64)
+        y_turned = keep.tile([P, N_CHUNKS, 4 * M], BF16, name="y_turned", align_bytes=64)
+        y_codes = keep.tile([P, N_CHUNKS, M], U32, name="y_codes", align_bytes=64)
+        y_scales = keep.tile([P, N_CHUNKS, M], U8, name="y_scales", align_bytes=64)
 
         def load_q(lo, hi):
             group = lo // WIDE_TILES
             base = group * WIDE_TILES
             nc.sync.dma_start(out=q_raw[:, lo:hi, :], in_=group_rows(q_rows, group)[:, lo - base : hi - base, :])
+
+        def load_keys(cols):
+            code_cols = slice(2 * cols.start, 2 * cols.stop)
+            nc.sync.dma_start(out=k_codes[:, code_cols].bitcast(I32), in_=keys_words[0][:, code_cols].bitcast(I32))
+            for quad in range(4):
+                rows = keys_scales[0][4 * quad : 4 * quad + 4, cols].bitcast(I32)
+                nc.sync.dma_start(
+                    out=k_scales[32 * quad : 32 * quad + 32, cols].bitcast(I32),
+                    in_=rows.unsqueeze(0).to_broadcast([8, 4, (cols.stop - cols.start) // 4]),
+                )
 
         def load_offsets(group, cols):
             heads, copies = GROUPS[group]
@@ -108,74 +104,71 @@ def tile_causal_sigmoid_attention_weights_g4_kernel(
             heads, copies = GROUPS[group]
             shape = [heads.stop - heads.start, copies, 1]
             with nc.allow_non_contiguous_dma(reason="one head scale for each partition"):
-                nc.sync.dma_start(out=head_scale[group][:], in_=scale[heads].unsqueeze(1).unsqueeze(2).to_broadcast(shape))
-
-        def load_keys(cols):
-            two = slice(2 * cols.start, 2 * cols.stop)
-            nc.sync.dma_start(out=k_codes[:, two].bitcast(I32), in_=keys_words[0][:, two].bitcast(I32))
-            for quad in range(4):
-                rows = keys_scales[0][4 * quad : 4 * quad + 4, cols].bitcast(I32)
                 nc.sync.dma_start(
-                    out=k_scales[32 * quad : 32 * quad + 32, cols].bitcast(I32),
-                    in_=rows.unsqueeze(0).to_broadcast([8, 4, (cols.stop - cols.start) // 4]),
+                    out=head_scale[group][:], in_=scale[heads].unsqueeze(1).unsqueeze(2).to_broadcast(shape)
                 )
 
-        first = slice(CHUNK_ORDER[0] * CHUNK, S)
-        rest = slice(0, CHUNK_ORDER[0] * CHUNK)
-        nc.vector.memset(warm[:], 0.0)
-        nc.scalar.activation(out=warm_out[:], in_=warm[:], func=ACT.Sigmoid)
+        nc.vector.memset(warm_in[:], 0.0)
+        nc.scalar.activation(out=warm_out[:], in_=warm_in[:], func=ACT.Sigmoid)
+
+        first_keys = slice(SWEEP_CHUNK[0] * CHUNK, S)
+        other_keys = slice(0, SWEEP_CHUNK[0] * CHUNK)
         load_q(0, 2)
-        load_keys(first)
-        load_offsets(0, first)
-        load_scale(0)
         load_q(2, 4)
-        load_offsets(1, first)
-        load_q(4, 8)
-        load_q(8, 10)
+        load_keys(first_keys)
+        load_offsets(0, first_keys)
+        load_scale(0)
+        load_q(4, WIDE_TILES)
+        load_offsets(1, first_keys)
+        load_q(WIDE_TILES, TILES)
         load_scale(1)
-        load_keys(rest)
-        load_offsets(0, rest)
-        load_offsets(1, rest)
+        load_keys(other_keys)
+        load_offsets(0, other_keys)
+        load_offsets(1, other_keys)
 
         make_identity(nc, ident[:])
-        nc.gpsimd.iota(row_index[:, 0:8, :], pattern=[[1, 8], [0, T]], base=0, channel_multiplier=8)
-        nc.gpsimd.iota(row_index[:, 8:10, :], pattern=[[1, 2], [0, T]], base=0, channel_multiplier=2)
-        nc.gpsimd.iota(key_pos[:], pattern=[[0, TILES], [1, T]], base=0, channel_multiplier=0,
-                       allow_small_or_imprecise_dtypes=True)
+        for tiles in (slice(0, WIDE_TILES), slice(WIDE_TILES, TILES)):
+            n = tiles.stop - tiles.start
+            nc.gpsimd.iota(row_index[:, tiles, :], pattern=[[1, n], [0, T]], base=0, channel_multiplier=n)
+        nc.gpsimd.iota(
+            key_pos[:], pattern=[[0, TILES], [1, T]], base=0, channel_multiplier=0, allow_small_or_imprecise_dtypes=True
+        )
         nc.vector.tensor_scalar(out=token[:], in0=row_index[:], scalar1=T - 1, scalar2=None, op0=ALU.bitwise_and)
         nc.vector.tensor_tensor(out=unseen[:], in0=token[:], in1=key_pos[:], op=ALU.is_lt)
 
         def mask_offsets(group):
             tiles = (slice(0, WIDE_TILES), slice(WIDE_TILES, TILES))[group]
             nc.vector.scalar_tensor_tensor(
-                out=off_masked[:, tiles, :], in0=unseen[:, tiles, :], scalar=MASKED,
+                out=off_masked[:, tiles, :],
+                in0=unseen[:, tiles, :],
+                scalar=MASKED,
                 in1=off[group][:, S - T : S].unsqueeze(1).to_broadcast([P, tiles.stop - tiles.start, T]),
-                op0=ALU.mult, op1=ALU.add,
+                op0=ALU.mult,
+                op1=ALU.add,
             )
 
-        q_grouped, score_banks, z_of, y_of, yb_of, turned = {}, {}, {}, {}, {}, {}
+        q_grouped, score_banks, z_of, y_of, y_rounded, y_banks = {}, {}, {}, {}, {}, {}
 
-        def turn_q(lo):
-            n = 1 if lo < 2 else 2
+        def turn_q(lo, n):
             bank = psum.tile([P, n, 2, P], F32, name="q_bank", tag="turn", bufs=4)
             for c in range(n):
                 words = q_raw[:, lo + c, :].bitcast(F32)
                 for u in range(2):
                     nc.tensor.transpose(bank[:, c, u, :], words[:, u : D // 2 : 2], ident[:])
             grouped = work.tile([P, n * 4 * P], BF16, name="q_grouped", tag="q_grouped", bufs=3, align_bytes=64)
-            copy = nc.vector.tensor_copy if lo == 0 else nc.scalar.copy
-            copy(out=grouped[:].bitcast(F32).rearrange("p (c r u) -> p c r u", c=n, u=2),
-                 in_=bank[:].rearrange("p c u r -> p c r u"))
+            nc.scalar.copy(
+                out=grouped[:].bitcast(F32).rearrange("p (c r u) -> p c r u", c=n, u=2),
+                in_=bank[:].rearrange("p c u r -> p c r u"),
+            )
             q_grouped[lo] = grouped
 
-        def quantize_q(lo):
-            n = 1 if lo < 2 else 2
-            nc.vector.quantize_mx(out=q_codes[:, lo * P : (lo + n) * P].bitcast(FP8X4),
-                                  scales=q_scales[:, lo * P : (lo + n) * P], in_=q_grouped[lo][:])
+        def quantize_q(lo, n):
+            cols = slice(lo * P, (lo + n) * P)
+            nc.vector.quantize_mx(out=q_codes[:, cols].bitcast(FP8X4), scales=q_scales[:, cols], in_=q_grouped[lo][:])
 
         def scores(step):
-            for i, (tile, pos) in enumerate(step_items(step)):
-                g = CHUNK_ORDER[pos]
+            tile, g0 = step % TILES, SWEEP_CHUNK[step // TILES]
+            for g in (g0, g0 + 1):
                 bank = psum.tile([P, CHUNK], F32, name="score_bank", tag="score", bufs=4)
                 nc.tensor.matmul_mx(
                     out=bank[:],
@@ -186,123 +179,133 @@ def tile_causal_sigmoid_attention_weights_g4_kernel(
                     start=True,
                     stop=True,
                 )
-                score_banks[step, i] = bank
+                score_banks[step, g] = bank
 
         def affine(step):
-            z = work.tile([P, 2, CHUNK], F32, name="z", tag="z", bufs=5)
-            for i, (tile, pos) in enumerate(step_items(step)):
-                g, group = CHUNK_ORDER[pos], tile // WIDE_TILES
+            tile, g0 = step % TILES, SWEEP_CHUNK[step // TILES]
+            group = tile // WIDE_TILES
+            z = work.tile([P, SPAN], F32, name="z", tag="z", bufs=6)
+            for g in (g0, g0 + 1):
                 plain = CHUNK - T if g == N_CHUNKS - 1 else CHUNK
-                nc.vector.scalar_tensor_tensor(
-                    out=z[:, i, 0:plain], in0=score_banks[step, i][:, 0:plain], scalar=head_scale[group][:],
-                    in1=off[group][:, g * CHUNK : g * CHUNK + plain], op0=ALU.mult, op1=ALU.add,
-                )
+                parts = [(0, plain, off[group][:, g * CHUNK : g * CHUNK + plain])]
                 if plain < CHUNK:
+                    parts.append((plain, CHUNK, off_masked[:, tile, :]))
+                for lo, hi, offsets in parts:
                     nc.vector.scalar_tensor_tensor(
-                        out=z[:, i, plain:CHUNK], in0=score_banks[step, i][:, plain:CHUNK],
-                        scalar=head_scale[group][:], in1=off_masked[:, tile, :], op0=ALU.mult, op1=ALU.add,
+                        out=z[:, (g - g0) * CHUNK + lo : (g - g0) * CHUNK + hi],
+                        in0=score_banks[step, g][:, lo:hi],
+                        scalar=head_scale[group][:],
+                        in1=offsets,
+                        op0=ALU.mult,
+                        op1=ALU.add,
                     )
             z_of[step] = z
 
         def sigmoid(step):
-            (tile, pos), (last_tile, last_pos) = step_items(step)
+            tile, g0 = step % TILES, SWEEP_CHUNK[step // TILES]
             group = tile // WIDE_TILES
-            base = group * WIDE_TILES
-            keys = slice(CHUNK_ORDER[pos] * CHUNK, (CHUNK_ORDER[last_pos] + 1) * CHUNK)
-            dst = group_rows(y_rows, group)[:, tile - base : last_tile - base + 1, keys]
-            y = work.tile([P, 2 * CHUNK], F32, name="y", tag="y", bufs=6)
-            nc.scalar.activation(out=y[:], in_=z_of[step][:].rearrange("p i n -> p (i n)"), func=ACT.Sigmoid)
-            nc.sync.dma_start(out=dst, in_=y[:].rearrange("p (c n) -> p c n", c=last_tile - tile + 1))
+            y = work.tile([P, SPAN], F32, name="y", tag="y", bufs=8)
+            nc.scalar.activation(out=y[:], in_=z_of[step][:], func=ACT.Sigmoid)
+            dst = group_rows(y_rows, group)[:, tile - group * WIDE_TILES, g0 * CHUNK : g0 * CHUNK + SPAN]
+            nc.sync.dma_start(out=dst, in_=y[:])
             y_of[step] = y
 
         def round_y(step):
-            yb = work.tile([P, 2 * CHUNK], BF16, name="yb", tag="yb", bufs=6, align_bytes=64)
+            rounded = work.tile([P, SPAN], BF16, name="rounded", tag="rounded", bufs=5, align_bytes=64)
             if step in VECTOR_ROUNDS:
-                nc.vector.tensor_copy(out=yb[:].rearrange("p (u r e) -> p u r e", u=2, e=2),
-                                      in_=y_of[step][:].rearrange("p (r u e) -> p u r e", u=2, e=2))
+                nc.vector.tensor_copy(out=rounded[:], in_=y_of[step][:])
             else:
-                nc.gpsimd.tensor_scalar(out=yb[:], in0=y_of[step][:], scalar1=1.0, scalar2=0.0,
-                                        op0=ALU.mult, op1=ALU.add)
-            yb_of[step] = yb
+                nc.gpsimd.tensor_scalar(
+                    out=rounded[:], in0=y_of[step][:], scalar1=1.0, scalar2=0.0, op0=ALU.mult, op1=ALU.add
+                )
+            y_rounded[step] = rounded
 
         def turn_y(step):
-            words = yb_of[step][:].bitcast(F32)
-            for i, (tile, pos) in enumerate(step_items(step)):
-                if tile % 2 == 0:
-                    turned[pos, tile // 2] = psum.tile([P, 2, 2, P], F32, name="y_bank", tag="turn", bufs=4)
-                bank = turned[pos, tile // 2]
+            words = y_rounded[step][:].bitcast(F32)
+            for half in range(2):
+                index = step - step % 2 + half
+                if step % 2 == 0:
+                    y_banks[index] = psum.tile([P, 2, 2, P], F32, name="y_bank", tag="turn", bufs=4)
                 for u in range(2):
-                    if step in VECTOR_ROUNDS:
-                        src = words[:, (2 * u + i) * P : (2 * u + i + 1) * P]
-                    else:
-                        src = words[:, 2 * i * P + u : 2 * (i + 1) * P : 2]
-                    nc.tensor.transpose(bank[:, tile % 2, u, :], src, ident[:])
+                    src = words[:, half * CHUNK // 2 + u : (half + 1) * CHUNK // 2 : 2]
+                    nc.tensor.transpose(y_banks[index][:, step % 2, u, :], src, ident[:])
 
         def copy_y(index):
-            pos, pair = banks_in_order[index]
-            dst = yt[:].bitcast(F32)[:, 2 * pos * M : 2 * (pos + 1) * M]
-            if pair < PAIRS - 1:
-                dst = dst[:, 0 : 2 * M_WIDE].rearrange("p (r w) -> p r w", w=16)[:, :, 4 * pair : 4 * pair + 4]
+            c, g = index % TILES - index % 2, SWEEP_CHUNK[index // TILES] + index % 2
+            words = y_turned[:, g, :].bitcast(F32)
+            if c < WIDE_TILES:
+                dst = words[:, 0 : 2 * M_WIDE].rearrange("p (r w) -> p r w", r=P)[:, :, 2 * c : 2 * c + 4]
             else:
-                dst = dst[:, 2 * M_WIDE : 2 * M].rearrange("p (r w) -> p r w", w=4)
+                dst = words[:, 2 * M_WIDE : 2 * M].rearrange("p (r w) -> p r w", r=P)
             copy = nc.vector.tensor_copy if index in VECTOR_COPIES else nc.scalar.copy
-            copy(out=dst, in_=turned[pos, pair][:].rearrange("p c u r -> p r (c u)"))
+            copy(out=dst, in_=y_banks[index][:].rearrange("p c u r -> p r (c u)"))
 
-        def quantize_y(col, n):
-            nc.vector.quantize_mx(out=y_codes[:, col : col + n].bitcast(FP8X4), scales=y_scales[:, col : col + n],
-                                  in_=yt[:, 4 * col : 4 * (col + n)])
-            lo = col
-            while lo < col + n:
-                pos = lo // M
-                hi = min(col + n, (pos + 1) * M)
-                dst = out_1[CHUNK_ORDER[pos]].rearrange("p m t -> p (m t)").bitcast(I32)
-                nc.sync.dma_start(out=dst[:, lo - pos * M : hi - pos * M], in_=y_codes[:, lo:hi].bitcast(I32))
-                lo = hi
-            p1 = (col + n) // (2 * M) * 2
-            if p1 > col // (2 * M) * 2:
-                p0 = p1 - 2
-                g0 = CHUNK_ORDER[p0]
-                for quad in range(4):
-                    queue = nc.scalar if (p1 == N_CHUNKS and quad % 2) else nc.sync
-                    queue.dma_start(
-                        out=out_2[g0 : g0 + 2, 4 * quad : 4 * quad + 4, :].rearrange("g r m -> r g m").bitcast(I32),
-                        in_=y_scales[32 * quad : 32 * quad + 4, p0 * M : p1 * M].bitcast(I32).rearrange(
-                            "r (g m) -> r g m", g=2),
-                    )
+        def store_codes(chunks, cols):
+            nc.sync.dma_start(out=code_words[:, chunks, cols], in_=y_codes[:, chunks, cols].bitcast(I32))
 
-        turn_q(0)
-        turn_q(1)
-        quantize_q(0)
+        def store_scales(chunks, queues):
+            for quad in range(4):
+                queues[quad % len(queues)].dma_start(
+                    out=out_2[chunks, 4 * quad : 4 * quad + 4, :].rearrange("g r m -> r g m").bitcast(I32),
+                    in_=y_scales[32 * quad : 32 * quad + 4, chunks, :].bitcast(I32),
+                )
+
+        def quantize_y(sweep, call):
+            g0 = SWEEP_CHUNK[sweep]
+            g = g0 + call % 2
+            cols = slice(0, M_WIDE) if call < 2 else slice(M_WIDE, M)
+            nc.vector.quantize_mx(
+                out=y_codes[:, g, cols].bitcast(FP8X4),
+                scales=y_scales[:, g, cols],
+                in_=y_turned[:, g, 4 * cols.start : 4 * cols.stop],
+            )
+            both = slice(g0, g0 + 2)
+            if sweep < len(SWEEP_CHUNK) - 1:
+                if call >= 2:
+                    store_codes(slice(g, g + 1), slice(0, M))
+                if call == 3:
+                    store_scales(both, [nc.sync])
+            elif call < 2:
+                store_codes(slice(g, g + 1), cols)
+            elif call == 3:
+                store_scales(both, [nc.sync, nc.scalar])
+                store_codes(both, cols)
+
+        quant_start = [sweep * TILES + QUANT_LAG for sweep in range(len(SWEEP_CHUNK) - 1)] + [LAST_QUANT]
+
+        turn_q(0, 1)
+        turn_q(1, 1)
+        quantize_q(0, 1)
         scores(0)
-        for it in range(-1, max(QUANT_AT) + 1):
-            if it == 0:
-                mask_offsets(0)
-            if 0 <= it < STEPS:
+        quantize_q(1, 1)
+        turn_q(2, 2)
+        mask_offsets(0)
+        for it in range(LAST_QUANT + 4):
+            if it < STEPS:
                 affine(it)
-            if it == 1:
+            if it == WIDE_TILES // 2:
                 mask_offsets(1)
-            if it in Q_QUANT_AT:
-                quantize_q(Q_QUANT_AT[it])
+            if it % 2 == 0 and it + 2 < TILES:
+                quantize_q(it + 2, 2)
             if it - VECTOR_COPY_LAG in VECTOR_COPIES:
                 copy_y(it - VECTOR_COPY_LAG)
             if it - VECTOR_ROUND_LAG in VECTOR_ROUNDS:
                 round_y(it - VECTOR_ROUND_LAG)
-            for at, (col, n) in zip(QUANT_AT, WINDOWS):
-                if at == it:
-                    quantize_y(col, n)
-            if 1 <= it + SCORE_LEAD < STEPS:
+            for sweep, start in enumerate(quant_start):
+                if 0 <= it - start < 4:
+                    quantize_y(sweep, it - start)
+            if it + SCORE_LEAD < STEPS:
                 scores(it + SCORE_LEAD)
-            if it in Q_TURN_AT:
-                turn_q(Q_TURN_AT[it])
-            step = it - SIGMOID_LAG
-            if 0 <= step < STEPS:
-                sigmoid(step)
-                if step not in VECTOR_ROUNDS:
-                    round_y(step)
+            if it % 2 == 1 and it + 3 < TILES:
+                turn_q(it + 3, 2)
+            if it < STEPS:
+                sigmoid(it)
+                if it not in VECTOR_ROUNDS:
+                    round_y(it)
             step = it - TURN_LAG
-            if WIDE_STEPS <= step < STEPS:
+            if PAIRED_TURNS <= step < STEPS:
                 turn_y(step)
-            elif 0 <= step < WIDE_STEPS and step % 2:
+            elif 0 <= step < PAIRED_TURNS and step % 2 == 1:
                 turn_y(step - 1)
                 turn_y(step)
             index = it - SCALAR_COPY_LAG

from contextlib import ExitStack

import concourse.mybir as mybir
from concourse.masks import make_identity

H, T, D, S = 40, 32, 512, 3072
M = H * T
FLOPS = 2 * M * D * S

F32 = mybir.dt.float32
BF16 = mybir.dt.bfloat16
I32 = mybir.dt.int32
U32 = mybir.dt.uint32
U8 = mybir.dt.uint8
FP8X4 = mybir.dt.float8_e4m3fn_x4
FP4X4 = mybir.dt.float4_e2m1fn_x4
ALU = mybir.AluOpType
ACT = mybir.ActivationFunctionType

P = 128
CHUNK = 512
N_CHUNKS = S // CHUNK
SPAN = 2 * CHUNK
TILES = M // P
WIDE_TILES = 8
M_WIDE = WIDE_TILES * P
STEPS = TILES * S // SPAN
GROUPS = ((slice(0, 32), 4), (slice(32, 40), 16))
SWEEP_CHUNK = (4, 0, 2)
MASKED = -(2.0**126)

SCORE_LEAD = 1
VECTOR_ROUND_LAG = 2
TURN_LAG = 3
SCALAR_COPY_LAG = 4
VECTOR_COPY_LAG = 6
QUANT_LAG = 12
LAST_QUANT = 33
PAIRED_TURNS = 26
VECTOR_ROUNDS = (2, 10, 20, 27, 28, 29)
VECTOR_COPIES = (2, 12, 22, 25)


def group_rows(rows, group):
    if group == 0:
        return rows[0:M_WIDE, :].rearrange("(p c) n -> p c n", c=WIDE_TILES)
    return rows[M_WIDE:M, :].rearrange("(p c) n -> p c n", c=TILES - WIDE_TILES)


def tile_causal_sigmoid_attention_weights_g4_kernel(
    tc, q, keys_words, keys_scales, scale, offset, out_0, out_1, out_2
):
    nc = tc.nc
    q_rows = q.rearrange("h i d -> (h i) d")
    y_rows = out_0.rearrange("h i j -> (h i) j")
    code_words = out_1.rearrange("g p m t -> p g (m t)").bitcast(I32)

    with ExitStack() as ctx:
        keep = ctx.enter_context(tc.tile_pool(name="keep", bufs=1))
        work = ctx.enter_context(tc.tile_pool(name="work", bufs=1))
        psum = ctx.enter_context(tc.psum_pool(name="psum", bufs=1))
        ctx.enter_context(tc.manual_schedule())

        ident = keep.tile([P, P], F32, name="ident")
        warm_in = keep.tile([P, 1], F32, name="warm_in")
        warm_out = keep.tile([P, 1], F32, name="warm_out")
        k_codes = keep.tile([P, 2 * S], U8, name="k_codes", align_bytes=64)
        k_scales = keep.tile([P, S], U8, name="k_scales", align_bytes=64)
        q_raw = keep.tile([P, TILES, D], BF16, name="q_raw", align_bytes=64)
        q_codes = keep.tile([P, M], U32, name="q_codes", align_bytes=64)
        q_scales = keep.tile([P, M], U8, name="q_scales", align_bytes=64)
        off = [keep.tile([P, S], BF16, name="off%d" % group, align_bytes=64) for group in range(2)]
        head_scale = [keep.tile([P, 1], BF16, name="head_scale%d" % group) for group in range(2)]
        row_index = keep.tile([P, TILES, T], I32, name="row_index")
        token = keep.tile([P, TILES, T], I32, name="token")
        key_pos = keep.tile([P, TILES, T], F32, name="key_pos")
        unseen = keep.tile([P, TILES, T], F32, name="unseen")
        off_masked = keep.tile([P, TILES, T], F32, name="off_masked")
        y_turned = keep.tile([P, N_CHUNKS, 4 * M], BF16, name="y_turned", align_bytes=64)
        y_codes = keep.tile([P, N_CHUNKS, M], U32, name="y_codes", align_bytes=64)
        y_scales = keep.tile([P, N_CHUNKS, M], U8, name="y_scales", align_bytes=64)

        def load_q(lo, hi):
            group = lo // WIDE_TILES
            base = group * WIDE_TILES
            nc.sync.dma_start(out=q_raw[:, lo:hi, :], in_=group_rows(q_rows, group)[:, lo - base : hi - base, :])

        def load_keys(cols):
            code_cols = slice(2 * cols.start, 2 * cols.stop)
            nc.sync.dma_start(out=k_codes[:, code_cols].bitcast(I32), in_=keys_words[0][:, code_cols].bitcast(I32))
            for quad in range(4):
                rows = keys_scales[0][4 * quad : 4 * quad + 4, cols].bitcast(I32)
                nc.sync.dma_start(
                    out=k_scales[32 * quad : 32 * quad + 32, cols].bitcast(I32),
                    in_=rows.unsqueeze(0).to_broadcast([8, 4, (cols.stop - cols.start) // 4]),
                )

        def load_offsets(group, cols):
            heads, copies = GROUPS[group]
            shape = [heads.stop - heads.start, copies, cols.stop - cols.start]
            nc.sync.dma_start(out=off[group][:, cols], in_=offset[heads, cols].unsqueeze(1).to_broadcast(shape))

        def load_scale(group):
            heads, copies = GROUPS[group]
            shape = [heads.stop - heads.start, copies, 1]
            with nc.allow_non_contiguous_dma(reason="one head scale for each partition"):
                nc.sync.dma_start(
                    out=head_scale[group][:], in_=scale[heads].unsqueeze(1).unsqueeze(2).to_broadcast(shape)
                )

        nc.vector.memset(warm_in[:], 0.0)
        nc.scalar.activation(out=warm_out[:], in_=warm_in[:], func=ACT.Sigmoid)

        first_keys = slice(SWEEP_CHUNK[0] * CHUNK, S)
        other_keys = slice(0, SWEEP_CHUNK[0] * CHUNK)
        load_q(0, 2)
        load_q(2, 4)
        load_keys(first_keys)
        load_offsets(0, first_keys)
        load_scale(0)
        load_q(4, WIDE_TILES)
        load_offsets(1, first_keys)
        load_q(WIDE_TILES, TILES)
        load_scale(1)
        load_keys(other_keys)
        load_offsets(0, other_keys)
        load_offsets(1, other_keys)

        make_identity(nc, ident[:])
        for tiles in (slice(0, WIDE_TILES), slice(WIDE_TILES, TILES)):
            n = tiles.stop - tiles.start
            nc.gpsimd.iota(row_index[:, tiles, :], pattern=[[1, n], [0, T]], base=0, channel_multiplier=n)
        nc.gpsimd.iota(
            key_pos[:], pattern=[[0, TILES], [1, T]], base=0, channel_multiplier=0, allow_small_or_imprecise_dtypes=True
        )
        nc.vector.tensor_scalar(out=token[:], in0=row_index[:], scalar1=T - 1, scalar2=None, op0=ALU.bitwise_and)
        nc.vector.tensor_tensor(out=unseen[:], in0=token[:], in1=key_pos[:], op=ALU.is_lt)

        def mask_offsets(group):
            tiles = (slice(0, WIDE_TILES), slice(WIDE_TILES, TILES))[group]
            nc.vector.scalar_tensor_tensor(
                out=off_masked[:, tiles, :],
                in0=unseen[:, tiles, :],
                scalar=MASKED,
                in1=off[group][:, S - T : S].unsqueeze(1).to_broadcast([P, tiles.stop - tiles.start, T]),
                op0=ALU.mult,
                op1=ALU.add,
            )

        q_grouped, score_banks, z_of, y_of, y_rounded, y_banks = {}, {}, {}, {}, {}, {}

        def turn_q(lo, n):
            bank = psum.tile([P, n, 2, P], F32, name="q_bank", tag="turn", bufs=4)
            for c in range(n):
                words = q_raw[:, lo + c, :].bitcast(F32)
                for u in range(2):
                    nc.tensor.transpose(bank[:, c, u, :], words[:, u : D // 2 : 2], ident[:])
            grouped = work.tile([P, n * 4 * P], BF16, name="q_grouped", tag="q_grouped", bufs=3, align_bytes=64)
            nc.scalar.copy(
                out=grouped[:].bitcast(F32).rearrange("p (c r u) -> p c r u", c=n, u=2),
                in_=bank[:].rearrange("p c u r -> p c r u"),
            )
            q_grouped[lo] = grouped

        def quantize_q(lo, n):
            cols = slice(lo * P, (lo + n) * P)
            nc.vector.quantize_mx(out=q_codes[:, cols].bitcast(FP8X4), scales=q_scales[:, cols], in_=q_grouped[lo][:])

        def scores(step):
            tile, g0 = step % TILES, SWEEP_CHUNK[step // TILES]
            for g in (g0, g0 + 1):
                bank = psum.tile([P, CHUNK], F32, name="score_bank", tag="score", bufs=4)
                nc.tensor.matmul_mx(
                    out=bank[:],
                    lhsT=q_codes[:, tile * P : (tile + 1) * P].bitcast(FP8X4),
                    lhsT_scale=q_scales[:, tile * P : (tile + 1) * P],
                    rhs=k_codes[:, 2 * g * CHUNK : 2 * (g + 1) * CHUNK].bitcast(FP4X4),
                    rhs_scale=k_scales[:, g * CHUNK : (g + 1) * CHUNK],
                    start=True,
                    stop=True,
                )
                score_banks[step, g] = bank

        def affine(step):
            tile, g0 = step % TILES, SWEEP_CHUNK[step // TILES]
            group = tile // WIDE_TILES
            z = work.tile([P, SPAN], F32, name="z", tag="z", bufs=6)
            for g in (g0, g0 + 1):
                plain = CHUNK - T if g == N_CHUNKS - 1 else CHUNK
                parts = [(0, plain, off[group][:, g * CHUNK : g * CHUNK + plain])]
                if plain < CHUNK:
                    parts.append((plain, CHUNK, off_masked[:, tile, :]))
                for lo, hi, offsets in parts:
                    nc.vector.scalar_tensor_tensor(
                        out=z[:, (g - g0) * CHUNK + lo : (g - g0) * CHUNK + hi],
                        in0=score_banks[step, g][:, lo:hi],
                        scalar=head_scale[group][:],
                        in1=offsets,
                        op0=ALU.mult,
                        op1=ALU.add,
                    )
            z_of[step] = z

        def sigmoid(step):
            tile, g0 = step % TILES, SWEEP_CHUNK[step // TILES]
            group = tile // WIDE_TILES
            y = work.tile([P, SPAN], F32, name="y", tag="y", bufs=8)
            nc.scalar.activation(out=y[:], in_=z_of[step][:], func=ACT.Sigmoid)
            dst = group_rows(y_rows, group)[:, tile - group * WIDE_TILES, g0 * CHUNK : g0 * CHUNK + SPAN]
            nc.sync.dma_start(out=dst, in_=y[:])
            y_of[step] = y

        def round_y(step):
            rounded = work.tile([P, SPAN], BF16, name="rounded", tag="rounded", bufs=5, align_bytes=64)
            if step in VECTOR_ROUNDS:
                nc.vector.tensor_copy(out=rounded[:], in_=y_of[step][:])
            else:
                nc.gpsimd.tensor_scalar(
                    out=rounded[:], in0=y_of[step][:], scalar1=1.0, scalar2=0.0, op0=ALU.mult, op1=ALU.add
                )
            y_rounded[step] = rounded

        def turn_y(step):
            words = y_rounded[step][:].bitcast(F32)
            for half in range(2):
                index = step - step % 2 + half
                if step % 2 == 0:
                    y_banks[index] = psum.tile([P, 2, 2, P], F32, name="y_bank", tag="turn", bufs=4)
                for u in range(2):
                    src = words[:, half * CHUNK // 2 + u : (half + 1) * CHUNK // 2 : 2]
                    nc.tensor.transpose(y_banks[index][:, step % 2, u, :], src, ident[:])

        def copy_y(index):
            c, g = index % TILES - index % 2, SWEEP_CHUNK[index // TILES] + index % 2
            words = y_turned[:, g, :].bitcast(F32)
            if c < WIDE_TILES:
                dst = words[:, 0 : 2 * M_WIDE].rearrange("p (r w) -> p r w", r=P)[:, :, 2 * c : 2 * c + 4]
            else:
                dst = words[:, 2 * M_WIDE : 2 * M].rearrange("p (r w) -> p r w", r=P)
            copy = nc.vector.tensor_copy if index in VECTOR_COPIES else nc.scalar.copy
            copy(out=dst, in_=y_banks[index][:].rearrange("p c u r -> p r (c u)"))

        def store_codes(chunks, cols):
            nc.sync.dma_start(out=code_words[:, chunks, cols], in_=y_codes[:, chunks, cols].bitcast(I32))

        def store_scales(chunks, queues):
            for quad in range(4):
                queues[quad % len(queues)].dma_start(
                    out=out_2[chunks, 4 * quad : 4 * quad + 4, :].rearrange("g r m -> r g m").bitcast(I32),
                    in_=y_scales[32 * quad : 32 * quad + 4, chunks, :].bitcast(I32),
                )

        def quantize_y(sweep, call):
            g0 = SWEEP_CHUNK[sweep]
            g = g0 + call % 2
            cols = slice(0, M_WIDE) if call < 2 else slice(M_WIDE, M)
            nc.vector.quantize_mx(
                out=y_codes[:, g, cols].bitcast(FP8X4),
                scales=y_scales[:, g, cols],
                in_=y_turned[:, g, 4 * cols.start : 4 * cols.stop],
            )
            both = slice(g0, g0 + 2)
            if sweep < len(SWEEP_CHUNK) - 1:
                if call >= 2:
                    store_codes(slice(g, g + 1), slice(0, M))
                if call == 3:
                    store_scales(both, [nc.sync])
            elif call < 2:
                store_codes(slice(g, g + 1), cols)
            elif call == 3:
                store_scales(both, [nc.sync, nc.scalar])
                store_codes(both, cols)

        quant_start = [sweep * TILES + QUANT_LAG for sweep in range(len(SWEEP_CHUNK) - 1)] + [LAST_QUANT]

        turn_q(0, 1)
        turn_q(1, 1)
        quantize_q(0, 1)
        scores(0)
        quantize_q(1, 1)
        turn_q(2, 2)
        mask_offsets(0)
        for it in range(LAST_QUANT + 4):
            if it < STEPS:
                affine(it)
            if it == WIDE_TILES // 2:
                mask_offsets(1)
            if it % 2 == 0 and it + 2 < TILES:
                quantize_q(it + 2, 2)
            if it - VECTOR_COPY_LAG in VECTOR_COPIES:
                copy_y(it - VECTOR_COPY_LAG)
            if it - VECTOR_ROUND_LAG in VECTOR_ROUNDS:
                round_y(it - VECTOR_ROUND_LAG)
            for sweep, start in enumerate(quant_start):
                if 0 <= it - start < 4:
                    quantize_y(sweep, it - start)
            if it + SCORE_LEAD < STEPS:
                scores(it + SCORE_LEAD)
            if it % 2 == 1 and it + 3 < TILES:
                turn_q(it + 3, 2)
            if it < STEPS:
                sigmoid(it)
                if it not in VECTOR_ROUNDS:
                    round_y(it)
            step = it - TURN_LAG
            if PAIRED_TURNS <= step < STEPS:
                turn_y(step)
            elif 0 <= step < PAIRED_TURNS and step % 2 == 1:
                turn_y(step - 1)
                turn_y(step)
            index = it - SCALAR_COPY_LAG
            if 0 <= index < STEPS and index not in VECTOR_COPIES:
                copy_y(index)
